import numpy as np
import ml_dtypes


def mxq(x, axis, fmt="e4m3"):
    dtype, down = {"e4m3": (ml_dtypes.float8_e4m3fn, 7), "e5m2": (ml_dtypes.float8_e5m2, 14)}[fmt]
    v = np.moveaxis(np.asarray(x, np.float32).astype(ml_dtypes.bfloat16).astype(np.float64), axis, -1)
    blocks = v.reshape(v.shape[:-1] + (-1, 32))
    amax = np.abs(blocks).max(-1, keepdims=True)
    byte = np.maximum(np.where(amax > 0, np.frexp(amax)[1] - 1 + 127, 0) - down, 1)
    scale = np.exp2(byte - 127.0)
    codes = (blocks / scale).astype(np.float32).astype(dtype).astype(np.float64)
    return np.moveaxis((codes * scale).reshape(v.shape), -1, axis)


WIDE = False


def mx_kscale(k, group=512):
    if not WIDE:
        return np.ones(k)
    levels = np.array([10, -10, 5, -5, 0])
    if group != 512:
        return np.exp2(np.random.permutation(np.resize(levels, k // group))).repeat(group)
    if k % 512:
        return np.exp2(np.random.permutation(np.resize(levels, k // 32))).repeat(32)
    a = np.empty((k // 512, 16))
    for p in range(k // 512):
        a[p, :8] = np.random.permutation(np.resize(levels, 8))
        for g in range(8):
            far = levels[np.abs(levels - a[p, g]) >= 10]
            a[p, g + 8] = far[np.random.randint(len(far))]
    return np.exp2(a.ravel()).repeat(32)


def f64(x):
    return np.asarray(x).astype(np.float64)


def striped(idx):
    return np.tile(np.asarray(idx).reshape(-1, 16).T, (8, 1)).astype(np.uint16)


def unstriped(offs):
    return offs[:16].T.reshape(-1).astype(np.int64)


H, KV, D, NQ, N = 2, 2, 256, 512, 1024
CAP = 2.0


def setup_inputs():
    n = np.random.standard_normal
    s = mx_kscale(D, 0)[:, None]
    u = mx_kscale(N)
    t = np.random.uniform(0.5, 2.0, N) * u
    v = n((KV, N, 128))
    v[:, :, 127] = 1.0
    return {
        "qT": (n((H, D, NQ)) * s * (0.70 / np.sqrt(D))).astype(np.float32),
        "kT": (n((KV, D, N)) / s).astype(np.float32),
        "t": t.reshape(N, 1).astype(np.float32),
        "v": (v / t[:, None]).astype(np.float32),
        "kb": (0.5 * n((N, 1))).astype(np.float32),
        "og": n((H, NQ, 128)).astype(np.float32),
    }


def reference(qT, kT, t, v, kb, og):
    a = mxq(f64(kT), 1, "e4m3").transpose(0, 2, 1) @ mxq(f64(qT), 1, "e4m3")
    a = a + f64(kb)
    a = CAP * np.tanh(a / CAP)
    p = np.square(np.maximum(a, 0.0))
    w = p * f64(t)
    y = mxq(w, 1, "e4m3").transpose(0, 2, 1) @ mxq(f64(v), 1, "e4m3")
    y = y / (y[:, :, 127:128] + 1.0)
    y = y / (1.0 + np.exp(-f64(og)))
    return y

@@ -1,0 +1,285 @@
+from contextlib import ExitStack
+
+import concourse.mybir as mybir
+
+H, D, NQ, N, E = 2, 256, 512, 1024, 128
+CAP = 2.0
+FLOPS = 2 * H * N * NQ * D + 2 * H * N * NQ * E
+
+F32 = mybir.dt.float32
+BF16 = mybir.dt.bfloat16
+U32 = mybir.dt.uint32
+U8 = mybir.dt.uint8
+FP8X4 = mybir.dt.float8_e4m3fn_x4
+ALU = mybir.AluOpType
+ACT = mybir.ActivationFunctionType
+
+P = 128
+PACK = 4
+ROWS = D // PACK
+PASS = P * PACK
+PASSES = N // PASS
+QT = 128
+BANK = 512
+SCORE_BANKS = 3
+Q_HALF = NQ // 2
+
+
+def tile_rows_a_relu2_kb_cap_gate_kernel(tc, qT, kT, t, v, kb, og, out):
+    nc = tc.nc
+    with ExitStack() as ctx:
+        sb = ctx.enter_context(tc.tile_pool(name="sb", bufs=1))
+        ps = ctx.enter_context(tc.psum_pool(name="ps", bufs=1))
+        ctx.enter_context(tc.manual_schedule())
+
+        def sbuf(name, shape, dtype):
+            return sb.tile(shape, dtype, name=name, align_bytes=64)
+
+        def load(queue, name, src):
+            raw = sbuf(name, list(src.shape), F32)
+            queue.dma_start(out=raw[:], in_=src)
+            return raw
+
+        def mx_pair(name, words):
+            return sbuf(name + "_codes", [P, words], U32), sbuf(name + "_scales", [P, words], U8)
+
+        def quantise(pair, first_word, src):
+            codes, scales = pair
+            cols = slice(first_word, first_word + src.shape[1] // PACK)
+            nc.vector.quantize_mx(out=codes[:, cols].bitcast(FP8X4), scales=scales[:, cols], in_=src)
+
+        def pair_walk_rows(rows):
+            return rows.rearrange("p j (c i) -> p c j i", i=2)
+
+        def pair_walk_words(words):
+            return words.rearrange("p (c i j) -> p c j i", i=2, j=PACK)
+
+        k_rows = kT.rearrange("h (p j) n -> (h p) j n", j=PACK)
+        q_rows = qT.rearrange("h (p j) n -> (h p) j n", j=PACK)
+        og_rows = og.rearrange("h (a p) e -> p (h a) e", p=P)
+        out_rows = out.rearrange("h (a p) e -> p (h a) e", p=P)
+        half = PASS // 2
+        t_col = load(nc.scalar, "t_col", t.rearrange("(g p j) o -> p g (j o)", p=P, j=PACK))
+        kb_col = load(nc.scalar, "kb_col", kb.rearrange("(g p j) o -> p g (j o)", p=P, j=PACK))
+        og_first = load(nc.scalar, "og_first", og_rows[:, 0:1, :])
+        k0a_raw = load(nc.sync, "k0a_raw", k_rows[:, :, 0:half])
+        k0b_raw = load(nc.sync, "k0b_raw", k_rows[:, :, half:PASS])
+        qa_raw = load(nc.sync, "qa_raw", q_rows[:, :, 0:Q_HALF])
+        qb_raw = load(nc.sync, "qb_raw", q_rows[:, :, Q_HALF:NQ])
+        k1_raw = load(nc.sync, "k1_raw", k_rows[:, :, PASS:N])
+        v_raw = load(nc.sync, "v_raw", v.rearrange("h (g p j) e -> p (h g) (j e)", p=P, j=PACK))
+        og_rest = load(nc.sync, "og_rest", og_rows[:, 1:, :])
+
+        small = [P, PASSES, PACK]
+        t_abs = sbuf("t_abs", small, F32)
+        t_rsqrt = sbuf("t_rsqrt", small, F32)
+        t_sign = sbuf("t_sign", small, F32)
+        bias = sbuf("bias", small, F32)
+        root = sbuf("root", small, F32)
+        near_one = sbuf("near_one", small, F32)
+        polish = sbuf("polish", small, F32)
+        factor = sbuf("factor", small, F32)
+        gate = sbuf("gate", [P, H * NQ // QT, E], F32)
+
+        k16 = [sbuf("k16_%d" % g, [P, PASS * PACK], BF16) for g in range(PASSES)]
+        k_mx = [mx_pair("k%d" % g, PASS) for g in range(PASSES)]
+        qa16 = sbuf("qa16", [P, Q_HALF * PACK], BF16)
+        qb16 = sbuf("qb16", [P, Q_HALF * PACK], BF16)
+        q_mx = mx_pair("q", NQ)
+        v16 = sbuf("v16", [P, H * PASSES * E * PACK], BF16)
+        v_mx = mx_pair("v", H * PASSES * E)
+        units = [(g, b) for g in range(PASSES) for b in range(2)]
+        w_mx = {u: mx_pair("w%d%d" % u, H * Q_HALF) for u in units}
+        capped = {u: [sbuf("cap%d%d_%d" % (u + (r,)), [P, H * Q_HALF], F32) for r in range(PACK)] for u in units}
+        scaled = {u: sbuf("rel%d%d" % u, [P, PACK, H * Q_HALF], F32) for u in units}
+        w16 = {u: sbuf("w16_%d%d" % u, [P, H * Q_HALF * PACK], BF16) for u in units}
+
+        score_banks = [[ps.tile([P, BANK], F32, name="s%d_%d" % (h, i)) for i in range(SCORE_BANKS)] for h in range(H)]
+        y_banks = [ps.tile([P, BANK], F32, name="y%d" % i) for i in range(2)]
+        banks_used = [[] for h in range(H)]
+
+        def deal_keys(g, raw, first_token):
+            s0, count = first_token // PACK, raw.shape[2] // PACK
+            dealt = k16[g][:].rearrange("p (r s j) -> p s r j", r=PACK, j=PACK)
+            nc.vector.tensor_copy(out=dealt[:, s0 : s0 + count, :, :], in_=raw[:].rearrange("p j (s r) -> p s r j", r=PACK))
+
+        def quantise_keys(g, r0, count):
+            quantise(k_mx[g], r0 * P, k16[g][:, r0 * PASS : (r0 + count) * PASS])
+
+        def interleave_queries(copy, dst, raw, q0, count):
+            copy(out=pair_walk_words(dst[:, q0 * PACK : (q0 + count) * PACK]), in_=pair_walk_rows(raw[:, :, q0 : q0 + count]))
+
+        def gates(b):
+            for h in range(H):
+                n0 = max(1, h * (NQ // QT) + b * (Q_HALF // QT))
+                n1 = h * (NQ // QT) + (b + 1) * (Q_HALF // QT)
+                nc.scalar.activation(out=gate[:, n0:n1, :], in_=og_rest[:, n0 - 1 : n1 - 1, :], func=ACT.Sigmoid)
+
+        def sign_values(h, g):
+            cols = slice((h * PASSES + g) * PASS, (h * PASSES + g + 1) * PASS)
+            nc.vector.tensor_tensor(
+                out=pair_walk_words(v16[:, cols]),
+                in0=pair_walk_rows(v_raw[:, h * PASSES + g, :].rearrange("p (j e) -> p j e", j=PACK)),
+                in1=t_sign[:, g, :].unsqueeze(1).unsqueeze(3).to_broadcast([P, E // 2, PACK, 2]),
+                op=ALU.mult,
+            )
+
+        def cap_scores(unit, h, r0):
+            g, b = unit
+            bank = score_banks[h][len(banks_used[h]) % SCORE_BANKS]
+            banks_used[h].append(unit)
+            rows = slice(h * ROWS, (h + 1) * ROWS)
+            for r in (r0, r0 + 1):
+                tokens = slice(r * P, (r + 1) * P)
+                for a in range(Q_HALF // QT):
+                    queries = slice(b * Q_HALF + a * QT, b * Q_HALF + (a + 1) * QT)
+                    at = (r - r0) * Q_HALF + a * QT
+                    nc.tensor.matmul_mx(
+                        out=bank[:, at : at + QT],
+                        lhsT=k_mx[g][0][rows, tokens].bitcast(FP8X4),
+                        lhsT_scale=k_mx[g][1][rows, tokens],
+                        rhs=q_mx[0][rows, queries].bitcast(FP8X4),
+                        rhs_scale=q_mx[1][rows, queries],
+                        start=True,
+                        stop=True,
+                    )
+            for r in (r0, r0 + 1):
+                at = (r - r0) * Q_HALF
+                nc.scalar.activation(
+                    out=capped[unit][r][:, h * Q_HALF : (h + 1) * Q_HALF], in_=bank[:, at : at + Q_HALF], func=ACT.Tanh,
+                    bias=bias[:, g, r : r + 1], scale=1.0 / CAP,
+                )
+
+        def cap_pair(unit, r0):
+            for h in range(H):
+                cap_scores(unit, h, r0)
+
+        def relu_scale(unit, r):
+            nc.vector.tensor_scalar(
+                out=scaled[unit][:, r, :], in0=capped[unit][r][:], scalar1=0.0,
+                scalar2=factor[:, unit[0], r : r + 1], op0=ALU.max, op1=ALU.mult,
+            )
+
+        def square(unit, c0, count, on_scalar):
+            words = pair_walk_words(w16[unit][:, c0 * PACK : (c0 + count) * PACK])
+            src = pair_walk_rows(scaled[unit][:, :, c0 : c0 + count])
+            if on_scalar:
+                nc.scalar.activation(out=words, in_=src, func=ACT.Square)
+            else:
+                nc.vector.tensor_tensor(out=words, in0=src, in1=src, op=ALU.mult)
+
+        def quantise_weights(unit, c0, count):
+            quantise(w_mx[unit], c0, w16[unit][:, c0 * PACK : (c0 + count) * PACK])
+
+        def weigh_values(b, i0, count, bank):
+            for i in range(i0, i0 + count):
+                h = i * QT // Q_HALF
+                cols = slice(i * QT, (i + 1) * QT)
+                for g in range(PASSES):
+                    values = slice((h * PASSES + g) * E, (h * PASSES + g + 1) * E)
+                    nc.tensor.matmul_mx(
+                        out=bank[:, i * E : (i + 1) * E],
+                        lhsT=w_mx[g, b][0][:, cols].bitcast(FP8X4),
+                        lhsT_scale=w_mx[g, b][1][:, cols],
+                        rhs=v_mx[0][:, values].bitcast(FP8X4),
+                        rhs_scale=v_mx[1][:, values],
+                        start=(g == 0),
+                        stop=(g == PASSES - 1),
+                    )
+
+        dens, recips = {}, {}
+
+        def denominators(b, i0, count, bank):
+            dens[b, i0] = sbuf("den%d_%d" % (b, i0), [P, count], F32)
+            sums = bank[:].rearrange("p (a e) -> p a e", e=E)[:, i0 : i0 + count, E - 1]
+            nc.vector.tensor_scalar(out=dens[b, i0][:], in0=sums, scalar1=1.0, scalar2=None, op0=ALU.add)
+
+        def reciprocals(b, i0):
+            recips[b, i0] = sbuf("rec%d_%d" % (b, i0), list(dens[b, i0].shape), F32)
+            nc.vector.reciprocal(out=recips[b, i0][:], in_=dens[b, i0][:])
+
+        def finish(b, first, i0, count, bank, queue):
+            res = sbuf("res%d_%d" % (b, i0), [P, count, E], F32)
+            n0 = (i0 * QT // Q_HALF) * (NQ // QT) + b * (Q_HALF // QT) + i0 % (Q_HALF // QT)
+            for i in range(i0, i0 + count):
+                nc.vector.scalar_tensor_tensor(
+                    out=res[:, i - i0, :], in0=bank[:, i * E : (i + 1) * E], scalar=recips[b, first][:, i - first : i - first + 1],
+                    in1=gate[:, n0 + i - i0, :], op0=ALU.mult, op1=ALU.mult,
+                )
+            queue.dma_start(out=out_rows[:, n0 : n0 + count, :], in_=res[:])
+
+        nc.scalar.activation(out=t_rsqrt[:], in_=t_col[:], func=ACT.Abs_reciprocal_sqrt)
+        nc.scalar.activation(out=t_abs[:], in_=t_col[:], func=ACT.Abs)
+        nc.scalar.activation(out=t_sign[:], in_=t_col[:], func=ACT.Sign)
+        nc.scalar.mul(out=bias[:], in_=kb_col[:], mul=1.0 / CAP)
+
+        nc.scalar.activation(out=gate[:, 0:1, :], in_=og_first[:], func=ACT.Sigmoid)
+
+        u0, u1, u2, u3 = units
+        ya, yb = y_banks
+
+        nc.vector.tensor_tensor(out=root[:], in0=t_abs[:], in1=t_rsqrt[:], op=ALU.mult)
+        deal_keys(0, k0a_raw, 0)
+        nc.vector.tensor_tensor(out=near_one[:], in0=root[:], in1=t_rsqrt[:], op=ALU.mult)
+        deal_keys(0, k0b_raw, half)
+        nc.vector.tensor_scalar(out=polish[:], in0=near_one[:], scalar1=-CAP / 2, scalar2=3 * CAP / 2, op0=ALU.mult, op1=ALU.add)
+        quantise_keys(0, 0, 4)
+        interleave_queries(nc.scalar.copy, qa16, qa_raw, 0, QT)
+        interleave_queries(nc.vector.tensor_copy, qa16, qa_raw, QT, QT)
+        nc.vector.tensor_tensor(out=factor[:], in0=root[:], in1=polish[:], op=ALU.mult)
+        quantise(q_mx, 0, qa16[:])
+        cap_pair(u0, 0)
+        cap_pair(u0, 2)
+        interleave_queries(nc.vector.tensor_copy, qb16, qb_raw, 0, Q_HALF)
+        quantise(q_mx, Q_HALF, qb16[:])
+        cap_pair(u1, 0)
+        cap_pair(u1, 2)
+        relu_scale(u0, 0)
+        relu_scale(u0, 1)
+        deal_keys(1, k1_raw, 0)
+        relu_scale(u0, 2)
+        relu_scale(u0, 3)
+        quantise_keys(1, 0, 4)
+        square(u0, 0, 512, True)
+        for r in range(4):
+            relu_scale(u1, r)
+        cap_pair(u2, 0)
+        cap_pair(u2, 2)
+        for h in range(H):
+            for g in range(PASSES):
+                sign_values(h, g)
+        quantise_weights(u0, 0, 512)
+        quantise(v_mx, 0, v16[:])
+        gates(0)
+        for r in range(4):
+            relu_scale(u2, r)
+        square(u2, 0, 384, True)
+        cap_pair(u3, 0)
+        cap_pair(u3, 2)
+        square(u1, 0, 512, False)
+        square(u2, 384, 128, False)
+        quantise_weights(u1, 0, 512)
+        quantise_weights(u2, 0, 512)
+        weigh_values(0, 0, 4, ya)
+        for r in range(4):
+            relu_scale(u3, r)
+        gates(1)
+        denominators(0, 0, 4, ya)
+        square(u3, 0, 128, True)
+        square(u3, 128, 128, True)
+        square(u3, 256, 128, True)
+        square(u3, 384, 128, False)
+        reciprocals(0, 0)
+        quantise_weights(u3, 0, 128)
+        finish(0, 0, 0, 2, ya, nc.sync)
+        quantise_weights(u3, 128, 128)
+        weigh_values(1, 0, 2, yb)
+        finish(0, 0, 2, 2, ya, nc.sync)
+        quantise_weights(u3, 256, 256)
+        weigh_values(1, 2, 2, ya)
+        denominators(1, 0, 2, yb)
+        reciprocals(1, 0)
+        denominators(1, 2, 2, ya)
+        finish(1, 0, 0, 2, yb, nc.sync)
+        reciprocals(1, 2)
+        finish(1, 2, 2, 2, ya, nc.scalar)

@@ -21,7 +21,7 @@ PASS = P * PACK
 PASSES = N // PASS
 QT = 128
 BANK = 512
-SCORE_BANKS = 3
+SCORE_BANKS = 2
 Q_HALF = NQ // 2
 
 
@@ -49,10 +49,10 @@ def tile_rows_a_relu2_kb_cap_gate_kernel(tc, qT, kT, t, v, kb, og, out):
             nc.vector.quantize_mx(out=codes[:, cols].bitcast(FP8X4), scales=scales[:, cols], in_=src)
 
         def pair_walk_rows(rows):
-            return rows.rearrange("p j (c i) -> p c j i", i=2)
+            return rows.rearrange("p j (c i) -> p c j i", i=4)
 
         def pair_walk_words(words):
-            return words.rearrange("p (c i j) -> p c j i", i=2, j=PACK)
+            return words.rearrange("p (c i j) -> p c j i", i=4, j=PACK)
 
         k_rows = kT.rearrange("h (p j) n -> (h p) j n", j=PACK)
         q_rows = qT.rearrange("h (p j) n -> (h p) j n", j=PACK)
@@ -60,13 +60,14 @@ def tile_rows_a_relu2_kb_cap_gate_kernel(tc, qT, kT, t, v, kb, og, out):
         out_rows = out.rearrange("h (a p) e -> p (h a) e", p=P)
         half = PASS // 2
         t_col = load(nc.scalar, "t_col", t.rearrange("(g p j) o -> p g (j o)", p=P, j=PACK))
-        kb_col = load(nc.scalar, "kb_col", kb.rearrange("(g p j) o -> p g (j o)", p=P, j=PACK))
         og_first = load(nc.scalar, "og_first", og_rows[:, 0:1, :])
         k0a_raw = load(nc.sync, "k0a_raw", k_rows[:, :, 0:half])
         k0b_raw = load(nc.sync, "k0b_raw", k_rows[:, :, half:PASS])
         qa_raw = load(nc.sync, "qa_raw", q_rows[:, :, 0:Q_HALF])
+        kb_col = load(nc.sync, "kb_col", kb.rearrange("(g p j) o -> p g (j o)", p=P, j=PACK))
         qb_raw = load(nc.sync, "qb_raw", q_rows[:, :, Q_HALF:NQ])
-        k1_raw = load(nc.sync, "k1_raw", k_rows[:, :, PASS:N])
+        k1a_raw = load(nc.sync, "k1a_raw", k_rows[:, :, PASS : PASS + half])
+        k1b_raw = load(nc.sync, "k1b_raw", k_rows[:, :, PASS + half : N])
         v_raw = load(nc.sync, "v_raw", v.rearrange("h (g p j) e -> p (h g) (j e)", p=P, j=PACK))
         og_rest = load(nc.sync, "og_rest", og_rows[:, 1:, :])
 
@@ -95,13 +96,13 @@ def tile_rows_a_relu2_kb_cap_gate_kernel(tc, qT, kT, t, v, kb, og, out):
         w16 = {u: sbuf("w16_%d%d" % u, [P, H * Q_HALF * PACK], BF16) for u in units}
 
         score_banks = [[ps.tile([P, BANK], F32, name="s%d_%d" % (h, i)) for i in range(SCORE_BANKS)] for h in range(H)]
-        y_banks = [ps.tile([P, BANK], F32, name="y%d" % i) for i in range(2)]
+        y_banks = [ps.tile([P, BANK], F32, name="y%d" % i) for i in range(4)]
         banks_used = [[] for h in range(H)]
 
         def deal_keys(g, raw, first_token):
             s0, count = first_token // PACK, raw.shape[2] // PACK
-            dealt = k16[g][:].rearrange("p (r s j) -> p s r j", r=PACK, j=PACK)
-            nc.vector.tensor_copy(out=dealt[:, s0 : s0 + count, :, :], in_=raw[:].rearrange("p j (s r) -> p s r j", r=PACK))
+            dealt = k16[g][:].rearrange("p (r s j) -> p s j r", r=PACK, j=PACK)
+            nc.vector.tensor_copy(out=dealt[:, s0 : s0 + count, :, :], in_=raw[:].rearrange("p j (s r) -> p s j r", r=PACK))
 
         def quantise_keys(g, r0, count):
             quantise(k_mx[g], r0 * P, k16[g][:, r0 * PASS : (r0 + count) * PASS])
@@ -109,31 +110,30 @@ def tile_rows_a_relu2_kb_cap_gate_kernel(tc, qT, kT, t, v, kb, og, out):
         def interleave_queries(copy, dst, raw, q0, count):
             copy(out=pair_walk_words(dst[:, q0 * PACK : (q0 + count) * PACK]), in_=pair_walk_rows(raw[:, :, q0 : q0 + count]))
 
-        def gates(b):
-            for h in range(H):
-                n0 = max(1, h * (NQ // QT) + b * (Q_HALF // QT))
-                n1 = h * (NQ // QT) + (b + 1) * (Q_HALF // QT)
-                nc.scalar.activation(out=gate[:, n0:n1, :], in_=og_rest[:, n0 - 1 : n1 - 1, :], func=ACT.Sigmoid)
-
         def sign_values(h, g):
             cols = slice((h * PASSES + g) * PASS, (h * PASSES + g + 1) * PASS)
             nc.vector.tensor_tensor(
                 out=pair_walk_words(v16[:, cols]),
                 in0=pair_walk_rows(v_raw[:, h * PASSES + g, :].rearrange("p (j e) -> p j e", j=PACK)),
-                in1=t_sign[:, g, :].unsqueeze(1).unsqueeze(3).to_broadcast([P, E // 2, PACK, 2]),
+                in1=t_sign[:, g, :].unsqueeze(1).unsqueeze(3).to_broadcast([P, E // 4, PACK, 4]),
                 op=ALU.mult,
             )
 
-        def cap_scores(unit, h, r0):
-            g, b = unit
+        def place(g, h, a):
+            if g == 0:
+                return (0, a // 2), h * Q_HALF + (a % 2) * QT
+            return (1, h), a * QT
+
+        def cap_scores(g, h, rs, a0, count):
             bank = score_banks[h][len(banks_used[h]) % SCORE_BANKS]
-            banks_used[h].append(unit)
+            banks_used[h].append(g)
             rows = slice(h * ROWS, (h + 1) * ROWS)
-            for r in (r0, r0 + 1):
+            width = count * QT
+            for n, r in enumerate(rs):
                 tokens = slice(r * P, (r + 1) * P)
-                for a in range(Q_HALF // QT):
-                    queries = slice(b * Q_HALF + a * QT, b * Q_HALF + (a + 1) * QT)
-                    at = (r - r0) * Q_HALF + a * QT
+                for a in range(count):
+                    queries = slice((a0 + a) * QT, (a0 + a + 1) * QT)
+                    at = n * width + a * QT
                     nc.tensor.matmul_mx(
                         out=bank[:, at : at + QT],
                         lhsT=k_mx[g][0][rows, tokens].bitcast(FP8X4),
@@ -143,44 +143,43 @@ def tile_rows_a_relu2_kb_cap_gate_kernel(tc, qT, kT, t, v, kb, og, out):
                         start=True,
                         stop=True,
                     )
-            for r in (r0, r0 + 1):
-                at = (r - r0) * Q_HALF
+            unit, c0 = place(g, h, a0)
+            for n, r in enumerate(rs):
                 nc.scalar.activation(
-                    out=capped[unit][r][:, h * Q_HALF : (h + 1) * Q_HALF], in_=bank[:, at : at + Q_HALF], func=ACT.Tanh,
-                    bias=bias[:, g, r : r + 1], scale=1.0 / CAP,
+                    out=capped[unit][r][:, c0 : c0 + width], in_=bank[:, n * width : (n + 1) * width],
+                    func=ACT.Tanh, bias=bias[:, g, r : r + 1], scale=1.0 / CAP,
                 )
 
-        def cap_pair(unit, r0):
-            for h in range(H):
-                cap_scores(unit, h, r0)
+        def relu_scale(unit, rs):
+            for r in rs:
+                nc.vector.tensor_scalar(
+                    out=scaled[unit][:, r, :], in0=capped[unit][r][:], scalar1=0.0,
+                    scalar2=factor[:, unit[0], r : r + 1], op0=ALU.max, op1=ALU.mult,
+                )
 
-        def relu_scale(unit, r):
-            nc.vector.tensor_scalar(
-                out=scaled[unit][:, r, :], in0=capped[unit][r][:], scalar1=0.0,
-                scalar2=factor[:, unit[0], r : r + 1], op0=ALU.max, op1=ALU.mult,
-            )
-
-        def square(unit, c0, count, on_scalar):
-            words = pair_walk_words(w16[unit][:, c0 * PACK : (c0 + count) * PACK])
-            src = pair_walk_rows(scaled[unit][:, :, c0 : c0 + count])
+        def square(on_scalar, g, h, a0, count):
+            unit, c0 = place(g, h, a0)
+            words = pair_walk_words(w16[unit][:, c0 * PACK : (c0 + count * QT) * PACK])
+            src = pair_walk_rows(scaled[unit][:, :, c0 : c0 + count * QT])
             if on_scalar:
                 nc.scalar.activation(out=words, in_=src, func=ACT.Square)
             else:
                 nc.vector.tensor_tensor(out=words, in0=src, in1=src, op=ALU.mult)
 
-        def quantise_weights(unit, c0, count):
-            quantise(w_mx[unit], c0, w16[unit][:, c0 * PACK : (c0 + count) * PACK])
+        def quantise_weights(g, h, a0, count):
+            unit, c0 = place(g, h, a0)
+            quantise(w_mx[unit], c0, w16[unit][:, c0 * PACK : (c0 + count * QT) * PACK])
 
-        def weigh_values(b, i0, count, bank):
-            for i in range(i0, i0 + count):
-                h = i * QT // Q_HALF
-                cols = slice(i * QT, (i + 1) * QT)
+        def weigh_values(h, a0, count, bank):
+            for a in range(a0, a0 + count):
                 for g in range(PASSES):
+                    unit, c0 = place(g, h, a)
+                    cols = slice(c0, c0 + QT)
                     values = slice((h * PASSES + g) * E, (h * PASSES + g + 1) * E)
                     nc.tensor.matmul_mx(
-                        out=bank[:, i * E : (i + 1) * E],
-                        lhsT=w_mx[g, b][0][:, cols].bitcast(FP8X4),
-                        lhsT_scale=w_mx[g, b][1][:, cols],
+                        out=bank[:, a * E : (a + 1) * E],
+                        lhsT=w_mx[unit][0][:, cols].bitcast(FP8X4),
+                        lhsT_scale=w_mx[unit][1][:, cols],
                         rhs=v_mx[0][:, values].bitcast(FP8X4),
                         rhs_scale=v_mx[1][:, values],
                         start=(g == 0),
@@ -189,97 +188,106 @@ def tile_rows_a_relu2_kb_cap_gate_kernel(tc, qT, kT, t, v, kb, og, out):
 
         dens, recips = {}, {}
 
-        def denominators(b, i0, count, bank):
-            dens[b, i0] = sbuf("den%d_%d" % (b, i0), [P, count], F32)
-            sums = bank[:].rearrange("p (a e) -> p a e", e=E)[:, i0 : i0 + count, E - 1]
-            nc.vector.tensor_scalar(out=dens[b, i0][:], in0=sums, scalar1=1.0, scalar2=None, op0=ALU.add)
+        def denominators(h, a0, count, bank):
+            dens[h, a0] = sbuf("den%d_%d" % (h, a0), [P, count], F32)
+            sums = bank[:].rearrange("p (a e) -> p a e", e=E)[:, a0 : a0 + count, E - 1]
+            nc.vector.tensor_scalar(out=dens[h, a0][:], in0=sums, scalar1=1.0, scalar2=None, op0=ALU.add)
 
-        def reciprocals(b, i0):
-            recips[b, i0] = sbuf("rec%d_%d" % (b, i0), list(dens[b, i0].shape), F32)
-            nc.vector.reciprocal(out=recips[b, i0][:], in_=dens[b, i0][:])
+        def reciprocals(h, a0):
+            recips[h, a0] = sbuf("rec%d_%d" % (h, a0), list(dens[h, a0].shape), F32)
+            nc.vector.reciprocal(out=recips[h, a0][:], in_=dens[h, a0][:])
 
-        def finish(b, first, i0, count, bank, queue):
-            res = sbuf("res%d_%d" % (b, i0), [P, count, E], F32)
-            n0 = (i0 * QT // Q_HALF) * (NQ // QT) + b * (Q_HALF // QT) + i0 % (Q_HALF // QT)
-            for i in range(i0, i0 + count):
+        def finish(h, a0, count, bank, queue):
+            res = sbuf("res%d_%d" % (h, a0), [P, count, E], F32)
+            n0 = h * (NQ // QT) + a0
+            for n in range(count):
                 nc.vector.scalar_tensor_tensor(
-                    out=res[:, i - i0, :], in0=bank[:, i * E : (i + 1) * E], scalar=recips[b, first][:, i - first : i - first + 1],
-                    in1=gate[:, n0 + i - i0, :], op0=ALU.mult, op1=ALU.mult,
+                    out=res[:, n, :], in0=bank[:, (a0 + n) * E : (a0 + n + 1) * E], scalar=recips[h, a0][:, n : n + 1],
+                    in1=gate[:, n0 + n, :], op0=ALU.mult, op1=ALU.mult,
                 )
             queue.dma_start(out=out_rows[:, n0 : n0 + count, :], in_=res[:])
 
         nc.scalar.activation(out=t_rsqrt[:], in_=t_col[:], func=ACT.Abs_reciprocal_sqrt)
         nc.scalar.activation(out=t_abs[:], in_=t_col[:], func=ACT.Abs)
         nc.scalar.activation(out=t_sign[:], in_=t_col[:], func=ACT.Sign)
-        nc.scalar.mul(out=bias[:], in_=kb_col[:], mul=1.0 / CAP)
 
         nc.scalar.activation(out=gate[:, 0:1, :], in_=og_first[:], func=ACT.Sigmoid)
 
-        u0, u1, u2, u3 = units
-        ya, yb = y_banks
+        ya, yb, yc, yd = y_banks
+        S, V = True, False
 
-        nc.vector.tensor_tensor(out=root[:], in0=t_abs[:], in1=t_rsqrt[:], op=ALU.mult)
         deal_keys(0, k0a_raw, 0)
-        nc.vector.tensor_tensor(out=near_one[:], in0=root[:], in1=t_rsqrt[:], op=ALU.mult)
         deal_keys(0, k0b_raw, half)
-        nc.vector.tensor_scalar(out=polish[:], in0=near_one[:], scalar1=-CAP / 2, scalar2=3 * CAP / 2, op0=ALU.mult, op1=ALU.add)
+        nc.vector.tensor_tensor(out=root[:], in0=t_abs[:], in1=t_rsqrt[:], op=ALU.mult)
         quantise_keys(0, 0, 4)
-        interleave_queries(nc.scalar.copy, qa16, qa_raw, 0, QT)
-        interleave_queries(nc.vector.tensor_copy, qa16, qa_raw, QT, QT)
-        nc.vector.tensor_tensor(out=factor[:], in0=root[:], in1=polish[:], op=ALU.mult)
+        nc.vector.tensor_tensor(out=near_one[:], in0=root[:], in1=t_rsqrt[:], op=ALU.mult)
+        interleave_queries(nc.scalar.copy, qa16, qa_raw, 0, 96)
+        nc.scalar.mul(out=bias[:], in_=kb_col[:], mul=1.0 / CAP)
+        interleave_queries(nc.vector.tensor_copy, qa16, qa_raw, 96, 160)
+        nc.vector.tensor_scalar(out=polish[:], in0=near_one[:], scalar1=-CAP / 2, scalar2=3 * CAP / 2, op0=ALU.mult, op1=ALU.add)
         quantise(q_mx, 0, qa16[:])
-        cap_pair(u0, 0)
-        cap_pair(u0, 2)
         interleave_queries(nc.vector.tensor_copy, qb16, qb_raw, 0, Q_HALF)
+        nc.vector.tensor_tensor(out=factor[:], in0=root[:], in1=polish[:], op=ALU.mult)
         quantise(q_mx, Q_HALF, qb16[:])
-        cap_pair(u1, 0)
-        cap_pair(u1, 2)
-        relu_scale(u0, 0)
-        relu_scale(u0, 1)
-        deal_keys(1, k1_raw, 0)
-        relu_scale(u0, 2)
-        relu_scale(u0, 3)
+        for a0, groups in ((0, ((0,), (1,), (2, 3))), (2, ((0, 1), (2, 3)))):
+            for rs in groups:
+                for h in range(H):
+                    cap_scores(0, h, rs, a0, 2)
+        deal_keys(1, k1a_raw, 0)
+        relu_scale((0, 0), (0, 1))
+        deal_keys(1, k1b_raw, half)
+        relu_scale((0, 0), (2,))
         quantise_keys(1, 0, 4)
-        square(u0, 0, 512, True)
-        for r in range(4):
-            relu_scale(u1, r)
-        cap_pair(u2, 0)
-        cap_pair(u2, 2)
-        for h in range(H):
-            for g in range(PASSES):
-                sign_values(h, g)
-        quantise_weights(u0, 0, 512)
-        quantise(v_mx, 0, v16[:])
-        gates(0)
-        for r in range(4):
-            relu_scale(u2, r)
-        square(u2, 0, 384, True)
-        cap_pair(u3, 0)
-        cap_pair(u3, 2)
-        square(u1, 0, 512, False)
-        square(u2, 384, 128, False)
-        quantise_weights(u1, 0, 512)
-        quantise_weights(u2, 0, 512)
-        weigh_values(0, 0, 4, ya)
-        for r in range(4):
-            relu_scale(u3, r)
-        gates(1)
-        denominators(0, 0, 4, ya)
-        square(u3, 0, 128, True)
-        square(u3, 128, 128, True)
-        square(u3, 256, 128, True)
-        square(u3, 384, 128, False)
+        for r in range(PACK):
+            for h in range(H):
+                cap_scores(1, h, (r,), 0, 4)
+        relu_scale((0, 0), (3,))
+        sign_values(0, 0)
+        square(V, 0, 0, 0, 2)
+        relu_scale((0, 1), (0, 1, 2, 3))
+        sign_values(0, 1)
+        relu_scale((1, 0), (0, 1))
+        square(V, 0, 1, 0, 2)
+        quantise(v_mx, 0, v16[:, 0:1024])
+        relu_scale((1, 0), (2, 3))
+        square(S, 0, 0, 2, 2)
+        nc.scalar.activation(out=gate[:, 1:, :], in_=og_rest[:], func=ACT.Sigmoid)
+        square(S, 1, 0, 0, 2)
+        square(S, 1, 0, 2, 2)
+        quantise_weights(0, 0, 0, 4)
+        sign_values(1, 0)
+        sign_values(1, 1)
+        relu_scale((1, 1), (0, 1, 2, 3))
+        quantise_weights(1, 0, 0, 2)
+        weigh_values(0, 0, 2, ya)
+        quantise_weights(0, 0, 2, 2)
+        quantise(v_mx, 256, v16[:, 1024:2048])
+        square(S, 1, 1, 0, 2)
+        denominators(0, 0, 2, ya)
+        quantise_weights(1, 0, 2, 2)
+        weigh_values(0, 2, 2, yb)
         reciprocals(0, 0)
-        quantise_weights(u3, 0, 128)
-        finish(0, 0, 0, 2, ya, nc.sync)
-        quantise_weights(u3, 128, 128)
-        weigh_values(1, 0, 2, yb)
-        finish(0, 0, 2, 2, ya, nc.sync)
-        quantise_weights(u3, 256, 256)
-        weigh_values(1, 2, 2, ya)
-        denominators(1, 0, 2, yb)
+        square(V, 0, 1, 2, 1)
+        square(S, 0, 1, 3, 1)
+        finish(0, 0, 2, ya, nc.sync)
+        denominators(0, 2, 2, yb)
+        quantise_weights(1, 1, 0, 2)
+        weigh_values(1, 0, 2, yc)
+        reciprocals(0, 2)
+        square(S, 1, 1, 2, 1)
+        square(S, 1, 1, 3, 1)
+        quantise_weights(0, 1, 2, 2)
+        finish(0, 2, 2, yb, nc.sync)
+        denominators(1, 0, 2, yc)
+        quantise_weights(1, 1, 2, 1)
+        weigh_values(1, 2, 1, yd)
         reciprocals(1, 0)
-        denominators(1, 2, 2, ya)
-        finish(1, 0, 0, 2, yb, nc.sync)
+        quantise_weights(1, 1, 3, 1)
+        weigh_values(1, 3, 1, ya)
+        finish(1, 0, 2, yc, nc.sync)
+        denominators(1, 2, 1, yd)
+        denominators(1, 3, 1, ya)
         reciprocals(1, 2)
-        finish(1, 2, 2, 2, ya, nc.scalar)
+        reciprocals(1, 3)
+        finish(1, 2, 1, yd, nc.sync)
+        finish(1, 3, 1, ya, nc.scalar)

@@ -16,6 +16,7 @@ ACT = mybir.ActivationFunctionType
 
 P = 128
 PACK = 4
+QUAD = 32
 ROWS = D // PACK
 PASS = P * PACK
 PASSES = N // PASS
@@ -58,18 +59,32 @@ def tile_rows_a_relu2_kb_cap_gate_kernel(tc, qT, kT, t, v, kb, og, out):
         q_rows = qT.rearrange("h (p j) n -> (h p) j n", j=PACK)
         og_rows = og.rearrange("h (a p) e -> p (h a) e", p=P)
         out_rows = out.rearrange("h (a p) e -> p (h a) e", p=P)
-        half = PASS // 2
-        t_col = load(nc.scalar, "t_col", t.rearrange("(g p j) o -> p g (j o)", p=P, j=PACK))
-        og_first = load(nc.scalar, "og_first", og_rows[:, 0:1, :])
-        k0a_raw = load(nc.sync, "k0a_raw", k_rows[:, :, 0:half])
-        k0b_raw = load(nc.sync, "k0b_raw", k_rows[:, :, half:PASS])
+        token_rows = sbuf("token_rows", [P, PASSES * P], F32)
+        for row, src in enumerate((t, kb)):
+            nc.sync.dma_start(
+                out=token_rows[row:P:QUAD, :].rearrange("x (g n) -> x g n", g=PASSES),
+                in_=src.rearrange("(g x n) o -> x g (n o)", g=PASSES, n=P),
+            )
+        k0_raw = load(nc.sync, "k0_raw", k_rows[:, :, 0:PASS])
         qa_raw = load(nc.sync, "qa_raw", q_rows[:, :, 0:Q_HALF])
-        kb_col = load(nc.sync, "kb_col", kb.rearrange("(g p j) o -> p g (j o)", p=P, j=PACK))
+        og_first = load(nc.sync, "og_first", og_rows[:, 0:1, :])
         qb_raw = load(nc.sync, "qb_raw", q_rows[:, :, Q_HALF:NQ])
-        k1a_raw = load(nc.sync, "k1a_raw", k_rows[:, :, PASS : PASS + half])
-        k1b_raw = load(nc.sync, "k1b_raw", k_rows[:, :, PASS + half : N])
+        k1_raw = load(nc.sync, "k1_raw", k_rows[:, :, PASS:N])
         v_raw = load(nc.sync, "v_raw", v.rearrange("h (g p j) e -> p (h g) (j e)", p=P, j=PACK))
         og_rest = load(nc.sync, "og_rest", og_rows[:, 1:, :])
+
+        token_dealt = sbuf("token_dealt", [P, PASSES * P], F32)
+        token_cols = sbuf("token_cols", [P, PASSES * P], F32)
+        nc.vector.memset(token_dealt[:], 0.0)
+        for first in range(0, P, QUAD):
+            live = slice(first, first + 2)
+            nc.vector.tensor_copy(
+                out=token_dealt[live, :].rearrange("x (g r c) -> x g r c", g=PASSES, r=PACK),
+                in_=token_rows[live, :].rearrange("x (g c r) -> x g r c", g=PASSES, r=PACK),
+            )
+        nc.vector.transpose(out=token_cols[:], in_=token_dealt[:])
+        by_row = token_cols[:].rearrange("p (g r i) -> p g r i", g=PASSES, r=PACK)
+        t_col, kb_col = by_row[:, :, :, 0], by_row[:, :, :, 1]
 
         small = [P, PASSES, PACK]
         t_abs = sbuf("t_abs", small, F32)
@@ -99,16 +114,19 @@ def tile_rows_a_relu2_kb_cap_gate_kernel(tc, qT, kT, t, v, kb, og, out):
         y_banks = [ps.tile([P, BANK], F32, name="y%d" % i) for i in range(4)]
         banks_used = [[] for h in range(H)]
 
-        def deal_keys(g, raw, first_token):
-            s0, count = first_token // PACK, raw.shape[2] // PACK
+        def deal_keys(copy, g, raw, s0, count):
             dealt = k16[g][:].rearrange("p (r s j) -> p s j r", r=PACK, j=PACK)
-            nc.vector.tensor_copy(out=dealt[:, s0 : s0 + count, :, :], in_=raw[:].rearrange("p j (s r) -> p s j r", r=PACK))
+            rows = raw[:].rearrange("p j (s r) -> p s j r", r=PACK)
+            copy(out=dealt[:, s0 : s0 + count, :, :], in_=rows[:, s0 : s0 + count, :, :])
 
         def quantise_keys(g, r0, count):
             quantise(k_mx[g], r0 * P, k16[g][:, r0 * PASS : (r0 + count) * PASS])
 
         def interleave_queries(copy, dst, raw, q0, count):
             copy(out=pair_walk_words(dst[:, q0 * PACK : (q0 + count) * PACK]), in_=pair_walk_rows(raw[:, :, q0 : q0 + count]))
+
+        def gates(n0, n1):
+            nc.scalar.activation(out=gate[:, n0:n1, :], in_=og_rest[:, n0 - 1 : n1 - 1, :], func=ACT.Sigmoid)
 
         def sign_values(h, g):
             cols = slice((h * PASSES + g) * PASS, (h * PASSES + g + 1) * PASS)
@@ -202,30 +220,30 @@ def tile_rows_a_relu2_kb_cap_gate_kernel(tc, qT, kT, t, v, kb, og, out):
             n0 = h * (NQ // QT) + a0
             for n in range(count):
                 nc.vector.scalar_tensor_tensor(
-                    out=res[:, n, :], in0=bank[:, (a0 + n) * E : (a0 + n + 1) * E], scalar=recips[h, a0][:, n : n + 1],
+                    out=res[:, n, :], in0=bank[:, (a0 + n) * E : (a0 + n + 1) * E], scalar=recips[h, a0 // 2 * 2][:, a0 % 2 + n : a0 % 2 + n + 1],
                     in1=gate[:, n0 + n, :], op0=ALU.mult, op1=ALU.mult,
                 )
             queue.dma_start(out=out_rows[:, n0 : n0 + count, :], in_=res[:])
 
-        nc.scalar.activation(out=t_rsqrt[:], in_=t_col[:], func=ACT.Abs_reciprocal_sqrt)
-        nc.scalar.activation(out=t_abs[:], in_=t_col[:], func=ACT.Abs)
-        nc.scalar.activation(out=t_sign[:], in_=t_col[:], func=ACT.Sign)
+        nc.scalar.activation(out=t_rsqrt[:], in_=t_col, func=ACT.Abs_reciprocal_sqrt)
+        nc.scalar.activation(out=t_abs[:], in_=t_col, func=ACT.Abs)
+        nc.scalar.activation(out=t_sign[:], in_=t_col, func=ACT.Sign)
 
-        nc.scalar.activation(out=gate[:, 0:1, :], in_=og_first[:], func=ACT.Sigmoid)
+        nc.scalar.mul(out=bias[:], in_=kb_col, mul=1.0 / CAP)
 
         ya, yb, yc, yd = y_banks
         S, V = True, False
 
-        deal_keys(0, k0a_raw, 0)
-        deal_keys(0, k0b_raw, half)
         nc.vector.tensor_tensor(out=root[:], in0=t_abs[:], in1=t_rsqrt[:], op=ALU.mult)
-        quantise_keys(0, 0, 4)
+        deal_keys(nc.vector.tensor_copy, 0, k0_raw, 0, 84)
+        deal_keys(nc.scalar.copy, 0, k0_raw, 84, 44)
+        nc.scalar.activation(out=gate[:, 0:1, :], in_=og_first[:], func=ACT.Sigmoid)
         nc.vector.tensor_tensor(out=near_one[:], in0=root[:], in1=t_rsqrt[:], op=ALU.mult)
-        interleave_queries(nc.scalar.copy, qa16, qa_raw, 0, 96)
-        nc.scalar.mul(out=bias[:], in_=kb_col[:], mul=1.0 / CAP)
-        interleave_queries(nc.vector.tensor_copy, qa16, qa_raw, 96, 160)
-        nc.vector.tensor_scalar(out=polish[:], in0=near_one[:], scalar1=-CAP / 2, scalar2=3 * CAP / 2, op0=ALU.mult, op1=ALU.add)
+        quantise_keys(0, 0, 2)
+        interleave_queries(nc.vector.tensor_copy, qa16, qa_raw, 0, Q_HALF)
+        quantise_keys(0, 2, 2)
         quantise(q_mx, 0, qa16[:])
+        nc.vector.tensor_scalar(out=polish[:], in0=near_one[:], scalar1=-CAP / 2, scalar2=3 * CAP / 2, op0=ALU.mult, op1=ALU.add)
         interleave_queries(nc.vector.tensor_copy, qb16, qb_raw, 0, Q_HALF)
         nc.vector.tensor_tensor(out=factor[:], in0=root[:], in1=polish[:], op=ALU.mult)
         quantise(q_mx, Q_HALF, qb16[:])
@@ -233,61 +251,57 @@ def tile_rows_a_relu2_kb_cap_gate_kernel(tc, qT, kT, t, v, kb, og, out):
             for rs in groups:
                 for h in range(H):
                     cap_scores(0, h, rs, a0, 2)
-        deal_keys(1, k1a_raw, 0)
         relu_scale((0, 0), (0, 1))
-        deal_keys(1, k1b_raw, half)
+        deal_keys(nc.vector.tensor_copy, 1, k1_raw, 0, 128)
         relu_scale((0, 0), (2,))
         quantise_keys(1, 0, 4)
         for r in range(PACK):
             for h in range(H):
                 cap_scores(1, h, (r,), 0, 4)
         relu_scale((0, 0), (3,))
-        sign_values(0, 0)
+        relu_scale((0, 1), (0,))
         square(V, 0, 0, 0, 2)
-        relu_scale((0, 1), (0, 1, 2, 3))
+        relu_scale((0, 1), (1, 2, 3))
+        sign_values(0, 0)
         sign_values(0, 1)
         relu_scale((1, 0), (0, 1))
         square(V, 0, 1, 0, 2)
         quantise(v_mx, 0, v16[:, 0:1024])
         relu_scale((1, 0), (2, 3))
         square(S, 0, 0, 2, 2)
-        nc.scalar.activation(out=gate[:, 1:, :], in_=og_rest[:], func=ACT.Sigmoid)
         square(S, 1, 0, 0, 2)
+        gates(1, 4)
         square(S, 1, 0, 2, 2)
         quantise_weights(0, 0, 0, 4)
         sign_values(1, 0)
-        sign_values(1, 1)
         relu_scale((1, 1), (0, 1, 2, 3))
         quantise_weights(1, 0, 0, 2)
         weigh_values(0, 0, 2, ya)
+        sign_values(1, 1)
         quantise_weights(0, 0, 2, 2)
-        quantise(v_mx, 256, v16[:, 1024:2048])
-        square(S, 1, 1, 0, 2)
         denominators(0, 0, 2, ya)
+        quantise(v_mx, 256, v16[:, 1024:2048])
+        reciprocals(0, 0)
+        square(S, 1, 1, 0, 2)
         quantise_weights(1, 0, 2, 2)
         weigh_values(0, 2, 2, yb)
-        reciprocals(0, 0)
-        square(V, 0, 1, 2, 1)
-        square(S, 0, 1, 3, 1)
         finish(0, 0, 2, ya, nc.sync)
-        denominators(0, 2, 2, yb)
+        square(S, 0, 1, 2, 2)
         quantise_weights(1, 1, 0, 2)
         weigh_values(1, 0, 2, yc)
-        reciprocals(0, 2)
-        square(S, 1, 1, 2, 1)
+        square(V, 1, 1, 2, 1)
         square(S, 1, 1, 3, 1)
+        gates(4, 8)
+        denominators(0, 2, 2, yb)
         quantise_weights(0, 1, 2, 2)
-        finish(0, 2, 2, yb, nc.sync)
+        reciprocals(0, 2)
         denominators(1, 0, 2, yc)
-        quantise_weights(1, 1, 2, 1)
-        weigh_values(1, 2, 1, yd)
+        quantise_weights(1, 1, 2, 2)
+        weigh_values(1, 2, 2, yd)
         reciprocals(1, 0)
-        quantise_weights(1, 1, 3, 1)
-        weigh_values(1, 3, 1, ya)
+        finish(0, 2, 2, yb, nc.sync)
         finish(1, 0, 2, yc, nc.sync)
-        denominators(1, 2, 1, yd)
-        denominators(1, 3, 1, ya)
+        denominators(1, 2, 2, yd)
         reciprocals(1, 2)
-        reciprocals(1, 3)
         finish(1, 2, 1, yd, nc.sync)
-        finish(1, 3, 1, ya, nc.scalar)
+        finish(1, 3, 1, yd, nc.scalar)

@@ -65,8 +65,8 @@ def tile_rows_a_relu2_kb_cap_gate_kernel(tc, qT, kT, t, v, kb, og, out):
                 out=token_rows[row:P:QUAD, :].rearrange("x (g n) -> x g n", g=PASSES),
                 in_=src.rearrange("(g x n) o -> x g (n o)", g=PASSES, n=P),
             )
-        k0_raw = load(nc.sync, "k0_raw", k_rows[:, :, 0:PASS])
         qa_raw = load(nc.sync, "qa_raw", q_rows[:, :, 0:Q_HALF])
+        k0_raw = load(nc.sync, "k0_raw", k_rows[:, :, 0:PASS])
         og_first = load(nc.sync, "og_first", og_rows[:, 0:1, :])
         qb_raw = load(nc.sync, "qb_raw", q_rows[:, :, Q_HALF:NQ])
         k1_raw = load(nc.sync, "k1_raw", k_rows[:, :, PASS:N])
@@ -104,26 +104,26 @@ def tile_rows_a_relu2_kb_cap_gate_kernel(tc, qT, kT, t, v, kb, og, out):
         q_mx = mx_pair("q", NQ)
         v16 = sbuf("v16", [P, H * PASSES * E * PACK], BF16)
         v_mx = mx_pair("v", H * PASSES * E)
-        units = [(g, b) for g in range(PASSES) for b in range(2)]
-        w_mx = {u: mx_pair("w%d%d" % u, H * Q_HALF) for u in units}
-        capped = {u: [sbuf("cap%d%d_%d" % (u + (r,)), [P, H * Q_HALF], F32) for r in range(PACK)] for u in units}
-        scaled = {u: sbuf("rel%d%d" % u, [P, PACK, H * Q_HALF], F32) for u in units}
-        w16 = {u: sbuf("w16_%d%d" % u, [P, H * Q_HALF * PACK], BF16) for u in units}
+        widths = {(0, 0): H * Q_HALF, (0, 1): H * Q_HALF, (1, 0): H * NQ}
+        w_mx = {u: mx_pair("w%d%d" % u, n) for u, n in widths.items()}
+        capped = {u: [sbuf("cap%d%d_%d" % (u + (r,)), [P, n], F32) for r in range(PACK)] for u, n in widths.items()}
+        scaled = {u: sbuf("rel%d%d" % u, [P, PACK, n], F32) for u, n in widths.items()}
+        w16 = {u: sbuf("w16_%d%d" % u, [P, n * PACK], BF16) for u, n in widths.items()}
 
         score_banks = [[ps.tile([P, BANK], F32, name="s%d_%d" % (h, i)) for i in range(SCORE_BANKS)] for h in range(H)]
         y_banks = [ps.tile([P, BANK], F32, name="y%d" % i) for i in range(4)]
         banks_used = [[] for h in range(H)]
 
-        def deal_keys(copy, g, raw, s0, count):
+        def deal_keys(g, raw, r0, count):
             dealt = k16[g][:].rearrange("p (r s j) -> p s j r", r=PACK, j=PACK)
             rows = raw[:].rearrange("p j (s r) -> p s j r", r=PACK)
-            copy(out=dealt[:, s0 : s0 + count, :, :], in_=rows[:, s0 : s0 + count, :, :])
+            nc.vector.tensor_copy(out=dealt[:, :, :, r0 : r0 + count], in_=rows[:, :, :, r0 : r0 + count])
 
         def quantise_keys(g, r0, count):
             quantise(k_mx[g], r0 * P, k16[g][:, r0 * PASS : (r0 + count) * PASS])
 
-        def interleave_queries(copy, dst, raw, q0, count):
-            copy(out=pair_walk_words(dst[:, q0 * PACK : (q0 + count) * PACK]), in_=pair_walk_rows(raw[:, :, q0 : q0 + count]))
+        def interleave_queries(dst, raw):
+            nc.vector.tensor_copy(out=pair_walk_words(dst[:]), in_=pair_walk_rows(raw[:]))
 
         def gates(n0, n1):
             nc.scalar.activation(out=gate[:, n0:n1, :], in_=og_rest[:, n0 - 1 : n1 - 1, :], func=ACT.Sigmoid)
@@ -140,7 +140,7 @@ def tile_rows_a_relu2_kb_cap_gate_kernel(tc, qT, kT, t, v, kb, og, out):
         def place(g, h, a):
             if g == 0:
                 return (0, a // 2), h * Q_HALF + (a % 2) * QT
-            return (1, h), a * QT
+            return (1, 0), h * NQ + a * QT
 
         def cap_scores(g, h, rs, a0, count):
             bank = score_banks[h][len(banks_used[h]) % SCORE_BANKS]
@@ -188,9 +188,9 @@ def tile_rows_a_relu2_kb_cap_gate_kernel(tc, qT, kT, t, v, kb, og, out):
             unit, c0 = place(g, h, a0)
             quantise(w_mx[unit], c0, w16[unit][:, c0 * PACK : (c0 + count * QT) * PACK])
 
-        def weigh_values(h, a0, count, bank):
+        def weigh_values(h, a0, count, bank, passes=(0, 1)):
             for a in range(a0, a0 + count):
-                for g in range(PASSES):
+                for g in passes:
                     unit, c0 = place(g, h, a)
                     cols = slice(c0, c0 + QT)
                     values = slice((h * PASSES + g) * E, (h * PASSES + g + 1) * E)
@@ -220,7 +220,7 @@ def tile_rows_a_relu2_kb_cap_gate_kernel(tc, qT, kT, t, v, kb, og, out):
             n0 = h * (NQ // QT) + a0
             for n in range(count):
                 nc.vector.scalar_tensor_tensor(
-                    out=res[:, n, :], in0=bank[:, (a0 + n) * E : (a0 + n + 1) * E], scalar=recips[h, a0 // 2 * 2][:, a0 % 2 + n : a0 % 2 + n + 1],
+                    out=res[:, n, :], in0=bank[:, (a0 + n) * E : (a0 + n + 1) * E], scalar=recips[h, a0][:, n : n + 1],
                     in1=gate[:, n0 + n, :], op0=ALU.mult, op1=ALU.mult,
                 )
             queue.dma_start(out=out_rows[:, n0 : n0 + count, :], in_=res[:])
@@ -230,29 +230,30 @@ def tile_rows_a_relu2_kb_cap_gate_kernel(tc, qT, kT, t, v, kb, og, out):
         nc.scalar.activation(out=t_sign[:], in_=t_col, func=ACT.Sign)
 
         nc.scalar.mul(out=bias[:], in_=kb_col, mul=1.0 / CAP)
+        nc.scalar.activation(out=gate[:, 0:1, :], in_=og_first[:], func=ACT.Sigmoid)
 
         ya, yb, yc, yd = y_banks
         S, V = True, False
 
+        interleave_queries(qa16, qa_raw)
         nc.vector.tensor_tensor(out=root[:], in0=t_abs[:], in1=t_rsqrt[:], op=ALU.mult)
-        deal_keys(nc.vector.tensor_copy, 0, k0_raw, 0, 84)
-        deal_keys(nc.scalar.copy, 0, k0_raw, 84, 44)
-        nc.scalar.activation(out=gate[:, 0:1, :], in_=og_first[:], func=ACT.Sigmoid)
-        nc.vector.tensor_tensor(out=near_one[:], in0=root[:], in1=t_rsqrt[:], op=ALU.mult)
-        quantise_keys(0, 0, 2)
-        interleave_queries(nc.vector.tensor_copy, qa16, qa_raw, 0, Q_HALF)
-        quantise_keys(0, 2, 2)
         quantise(q_mx, 0, qa16[:])
+        nc.vector.tensor_tensor(out=near_one[:], in0=root[:], in1=t_rsqrt[:], op=ALU.mult)
         nc.vector.tensor_scalar(out=polish[:], in0=near_one[:], scalar1=-CAP / 2, scalar2=3 * CAP / 2, op0=ALU.mult, op1=ALU.add)
-        interleave_queries(nc.vector.tensor_copy, qb16, qb_raw, 0, Q_HALF)
         nc.vector.tensor_tensor(out=factor[:], in0=root[:], in1=polish[:], op=ALU.mult)
+        deal_keys(0, k0_raw, 0, 2)
+        quantise_keys(0, 0, 1)
+        deal_keys(0, k0_raw, 2, 2)
+        quantise_keys(0, 1, 1)
+        quantise_keys(0, 2, 2)
+        interleave_queries(qb16, qb_raw)
         quantise(q_mx, Q_HALF, qb16[:])
         for a0, groups in ((0, ((0,), (1,), (2, 3))), (2, ((0, 1), (2, 3)))):
             for rs in groups:
                 for h in range(H):
                     cap_scores(0, h, rs, a0, 2)
         relu_scale((0, 0), (0, 1))
-        deal_keys(nc.vector.tensor_copy, 1, k1_raw, 0, 128)
+        deal_keys(1, k1_raw, 0, 4)
         relu_scale((0, 0), (2,))
         quantise_keys(1, 0, 4)
         for r in range(PACK):
@@ -264,44 +265,49 @@ def tile_rows_a_relu2_kb_cap_gate_kernel(tc, qT, kT, t, v, kb, og, out):
         relu_scale((0, 1), (1, 2, 3))
         sign_values(0, 0)
         sign_values(0, 1)
-        relu_scale((1, 0), (0, 1))
-        square(V, 0, 1, 0, 2)
-        quantise(v_mx, 0, v16[:, 0:1024])
+        relu_scale((1, 0), (0,))
+        sign_values(1, 0)
+        relu_scale((1, 0), (1,))
+        sign_values(1, 1)
         relu_scale((1, 0), (2, 3))
         square(S, 0, 0, 2, 2)
-        square(S, 1, 0, 0, 2)
-        gates(1, 4)
+        square(S, 0, 1, 0, 2)
         square(S, 1, 0, 2, 2)
+        square(S, 1, 1, 0, 2)
+        quantise(v_mx, 0, v16[:])
+        square(V, 1, 0, 0, 2)
         quantise_weights(0, 0, 0, 4)
-        sign_values(1, 0)
-        relu_scale((1, 1), (0, 1, 2, 3))
         quantise_weights(1, 0, 0, 2)
         weigh_values(0, 0, 2, ya)
-        sign_values(1, 1)
         quantise_weights(0, 0, 2, 2)
-        denominators(0, 0, 2, ya)
-        quantise(v_mx, 256, v16[:, 1024:2048])
-        reciprocals(0, 0)
-        square(S, 1, 1, 0, 2)
         quantise_weights(1, 0, 2, 2)
         weigh_values(0, 2, 2, yb)
-        finish(0, 0, 2, ya, nc.sync)
+        gates(1, 2)
         square(S, 0, 1, 2, 2)
         quantise_weights(1, 1, 0, 2)
         weigh_values(1, 0, 2, yc)
-        square(V, 1, 1, 2, 1)
-        square(S, 1, 1, 3, 1)
+        denominators(0, 0, 2, ya)
+        square(V, 1, 1, 3, 1)
+        square(S, 1, 1, 2, 1)
+        gates(2, 4)
         gates(4, 8)
+        reciprocals(0, 0)
         denominators(0, 2, 2, yb)
+        finish(0, 0, 2, ya, nc.sync)
         quantise_weights(0, 1, 2, 2)
+        weigh_values(1, 2, 1, yd, (0,))
+        weigh_values(1, 3, 1, ya, (0,))
         reciprocals(0, 2)
         denominators(1, 0, 2, yc)
         quantise_weights(1, 1, 2, 2)
-        weigh_values(1, 2, 2, yd)
+        weigh_values(1, 2, 1, yd, (1,))
+        weigh_values(1, 3, 1, ya, (1,))
         reciprocals(1, 0)
         finish(0, 2, 2, yb, nc.sync)
         finish(1, 0, 2, yc, nc.sync)
-        denominators(1, 2, 2, yd)
+        denominators(1, 2, 1, yd)
+        denominators(1, 3, 1, ya)
         reciprocals(1, 2)
+        reciprocals(1, 3)
         finish(1, 2, 1, yd, nc.sync)
-        finish(1, 3, 1, yd, nc.scalar)
+        finish(1, 3, 1, ya, nc.scalar)

from contextlib import ExitStack

import concourse.mybir as mybir

H, D, NQ, N, E = 2, 256, 512, 1024, 128
CAP = 2.0
FLOPS = 2 * H * N * NQ * D + 2 * H * N * NQ * E

F32 = mybir.dt.float32
BF16 = mybir.dt.bfloat16
U32 = mybir.dt.uint32
U8 = mybir.dt.uint8
FP8X4 = mybir.dt.float8_e4m3fn_x4
ALU = mybir.AluOpType
ACT = mybir.ActivationFunctionType

P = 128
PACK = 4
QUAD = 32
ROWS = D // PACK
PASS = P * PACK
PASSES = N // PASS
QT = 128
BANK = 512
SCORE_BANKS = 2
Q_HALF = NQ // 2


def tile_rows_a_relu2_kb_cap_gate_kernel(tc, qT, kT, t, v, kb, og, out):
    nc = tc.nc
    with ExitStack() as ctx:
        sb = ctx.enter_context(tc.tile_pool(name="sb", bufs=1))
        ps = ctx.enter_context(tc.psum_pool(name="ps", bufs=1))
        ctx.enter_context(tc.manual_schedule())

        def sbuf(name, shape, dtype):
            return sb.tile(shape, dtype, name=name, align_bytes=64)

        def load(queue, name, src):
            raw = sbuf(name, list(src.shape), F32)
            queue.dma_start(out=raw[:], in_=src)
            return raw

        def mx_pair(name, words):
            return sbuf(name + "_codes", [P, words], U32), sbuf(name + "_scales", [P, words], U8)

        def quantise(pair, first_word, src):
            codes, scales = pair
            cols = slice(first_word, first_word + src.shape[1] // PACK)
            nc.vector.quantize_mx(out=codes[:, cols].bitcast(FP8X4), scales=scales[:, cols], in_=src)

        def pair_walk_rows(rows):
            return rows.rearrange("p j (c i) -> p c j i", i=4)

        def pair_walk_words(words):
            return words.rearrange("p (c i j) -> p c j i", i=4, j=PACK)

        k_rows = kT.rearrange("h (p j) n -> (h p) j n", j=PACK)
        q_rows = qT.rearrange("h (p j) n -> (h p) j n", j=PACK)
        og_rows = og.rearrange("h (a p) e -> p (h a) e", p=P)
        out_rows = out.rearrange("h (a p) e -> p (h a) e", p=P)
        token_rows = sbuf("token_rows", [P, PASSES * P], F32)
        for row, src in enumerate((t, kb)):
            nc.sync.dma_start(
                out=token_rows[row:P:QUAD, :].rearrange("x (g n) -> x g n", g=PASSES),
                in_=src.rearrange("(g x n) o -> x g (n o)", g=PASSES, n=P),
            )
        qa_raw = load(nc.sync, "qa_raw", q_rows[:, :, 0:Q_HALF])
        k0_raw = load(nc.sync, "k0_raw", k_rows[:, :, 0:PASS])
        og_first = load(nc.sync, "og_first", og_rows[:, 0:1, :])
        qb_raw = load(nc.sync, "qb_raw", q_rows[:, :, Q_HALF:NQ])
        k1_raw = load(nc.sync, "k1_raw", k_rows[:, :, PASS:N])
        v_raw = load(nc.sync, "v_raw", v.rearrange("h (g p j) e -> p (h g) (j e)", p=P, j=PACK))
        og_rest = load(nc.sync, "og_rest", og_rows[:, 1:, :])

        token_dealt = sbuf("token_dealt", [P, PASSES * P], F32)
        token_cols = sbuf("token_cols", [P, PASSES * P], F32)
        nc.vector.memset(token_dealt[:], 0.0)
        for first in range(0, P, QUAD):
            live = slice(first, first + 2)
            nc.vector.tensor_copy(
                out=token_dealt[live, :].rearrange("x (g r c) -> x g r c", g=PASSES, r=PACK),
                in_=token_rows[live, :].rearrange("x (g c r) -> x g r c", g=PASSES, r=PACK),
            )
        nc.vector.transpose(out=token_cols[:], in_=token_dealt[:])
        by_row = token_cols[:].rearrange("p (g r i) -> p g r i", g=PASSES, r=PACK)
        t_col, kb_col = by_row[:, :, :, 0], by_row[:, :, :, 1]

        small = [P, PASSES, PACK]
        t_abs = sbuf("t_abs", small, F32)
        t_rsqrt = sbuf("t_rsqrt", small, F32)
        t_sign = sbuf("t_sign", small, F32)
        bias = sbuf("bias", small, F32)
        root = sbuf("root", small, F32)
        near_one = sbuf("near_one", small, F32)
        polish = sbuf("polish", small, F32)
        factor = sbuf("factor", small, F32)
        gate = sbuf("gate", [P, H * NQ // QT, E], F32)

        k16 = [sbuf("k16_%d" % g, [P, PASS * PACK], BF16) for g in range(PASSES)]
        k_mx = [mx_pair("k%d" % g, PASS) for g in range(PASSES)]
        qa16 = sbuf("qa16", [P, Q_HALF * PACK], BF16)
        qb16 = sbuf("qb16", [P, Q_HALF * PACK], BF16)
        q_mx = mx_pair("q", NQ)
        v16 = sbuf("v16", [P, H * PASSES * E * PACK], BF16)
        v_mx = mx_pair("v", H * PASSES * E)
        widths = {(0, 0): H * Q_HALF, (0, 1): H * Q_HALF, (1, 0): H * NQ}
        w_mx = {u: mx_pair("w%d%d" % u, n) for u, n in widths.items()}
        capped = {u: [sbuf("cap%d%d_%d" % (u + (r,)), [P, n], F32) for r in range(PACK)] for u, n in widths.items()}
        scaled = {u: sbuf("rel%d%d" % u, [P, PACK, n], F32) for u, n in widths.items()}
        w16 = {u: sbuf("w16_%d%d" % u, [P, n * PACK], BF16) for u, n in widths.items()}

        score_banks = [[ps.tile([P, BANK], F32, name="s%d_%d" % (h, i)) for i in range(SCORE_BANKS)] for h in range(H)]
        y_banks = [ps.tile([P, BANK], F32, name="y%d" % i) for i in range(4)]
        banks_used = [[] for h in range(H)]

        def deal_keys(g, raw, r0, count):
            dealt = k16[g][:].rearrange("p (r s j) -> p s j r", r=PACK, j=PACK)
            rows = raw[:].rearrange("p j (s r) -> p s j r", r=PACK)
            nc.vector.tensor_copy(out=dealt[:, :, :, r0 : r0 + count], in_=rows[:, :, :, r0 : r0 + count])

        def quantise_keys(g, r0, count):
            quantise(k_mx[g], r0 * P, k16[g][:, r0 * PASS : (r0 + count) * PASS])

        def interleave_queries(dst, raw):
            nc.vector.tensor_copy(out=pair_walk_words(dst[:]), in_=pair_walk_rows(raw[:]))

        def gates(n0, n1):
            nc.scalar.activation(out=gate[:, n0:n1, :], in_=og_rest[:, n0 - 1 : n1 - 1, :], func=ACT.Sigmoid)

        def sign_values(h, g):
            cols = slice((h * PASSES + g) * PASS, (h * PASSES + g + 1) * PASS)
            nc.vector.tensor_tensor(
                out=pair_walk_words(v16[:, cols]),
                in0=pair_walk_rows(v_raw[:, h * PASSES + g, :].rearrange("p (j e) -> p j e", j=PACK)),
                in1=t_sign[:, g, :].unsqueeze(1).unsqueeze(3).to_broadcast([P, E // 4, PACK, 4]),
                op=ALU.mult,
            )

        def place(g, h, a):
            if g == 0:
                return (0, a // 2), h * Q_HALF + (a % 2) * QT
            return (1, 0), h * NQ + a * QT

        def cap_scores(g, h, rs, a0, count):
            bank = score_banks[h][len(banks_used[h]) % SCORE_BANKS]
            banks_used[h].append(g)
            rows = slice(h * ROWS, (h + 1) * ROWS)
            width = count * QT
            for n, r in enumerate(rs):
                tokens = slice(r * P, (r + 1) * P)
                for a in range(count):
                    queries = slice((a0 + a) * QT, (a0 + a + 1) * QT)
                    at = n * width + a * QT
                    nc.tensor.matmul_mx(
                        out=bank[:, at : at + QT],
                        lhsT=k_mx[g][0][rows, tokens].bitcast(FP8X4),
                        lhsT_scale=k_mx[g][1][rows, tokens],
                        rhs=q_mx[0][rows, queries].bitcast(FP8X4),
                        rhs_scale=q_mx[1][rows, queries],
                        start=True,
                        stop=True,
                    )
            unit, c0 = place(g, h, a0)
            for n, r in enumerate(rs):
                nc.scalar.activation(
                    out=capped[unit][r][:, c0 : c0 + width], in_=bank[:, n * width : (n + 1) * width],
                    func=ACT.Tanh, bias=bias[:, g, r : r + 1], scale=1.0 / CAP,
                )

        def relu_scale(unit, rs):
            for r in rs:
                nc.vector.tensor_scalar(
                    out=scaled[unit][:, r, :], in0=capped[unit][r][:], scalar1=0.0,
                    scalar2=factor[:, unit[0], r : r + 1], op0=ALU.max, op1=ALU.mult,
                )

        def square(on_scalar, g, h, a0, count):
            unit, c0 = place(g, h, a0)
            words = pair_walk_words(w16[unit][:, c0 * PACK : (c0 + count * QT) * PACK])
            src = pair_walk_rows(scaled[unit][:, :, c0 : c0 + count * QT])
            if on_scalar:
                nc.scalar.activation(out=words, in_=src, func=ACT.Square)
            else:
                nc.vector.tensor_tensor(out=words, in0=src, in1=src, op=ALU.mult)

        def quantise_weights(g, h, a0, count):
            unit, c0 = place(g, h, a0)
            quantise(w_mx[unit], c0, w16[unit][:, c0 * PACK : (c0 + count * QT) * PACK])

        def weigh_values(h, a0, count, bank, passes=(0, 1)):
            for a in range(a0, a0 + count):
                for g in passes:
                    unit, c0 = place(g, h, a)
                    cols = slice(c0, c0 + QT)
                    values = slice((h * PASSES + g) * E, (h * PASSES + g + 1) * E)
                    nc.tensor.matmul_mx(
                        out=bank[:, a * E : (a + 1) * E],
                        lhsT=w_mx[unit][0][:, cols].bitcast(FP8X4),
                        lhsT_scale=w_mx[unit][1][:, cols],
                        rhs=v_mx[0][:, values].bitcast(FP8X4),
                        rhs_scale=v_mx[1][:, values],
                        start=(g == 0),
                        stop=(g == PASSES - 1),
                    )

        dens, recips = {}, {}

        def denominators(h, a0, count, bank):
            dens[h, a0] = sbuf("den%d_%d" % (h, a0), [P, count], F32)
            sums = bank[:].rearrange("p (a e) -> p a e", e=E)[:, a0 : a0 + count, E - 1]
            nc.vector.tensor_scalar(out=dens[h, a0][:], in0=sums, scalar1=1.0, scalar2=None, op0=ALU.add)

        def reciprocals(h, a0):
            recips[h, a0] = sbuf("rec%d_%d" % (h, a0), list(dens[h, a0].shape), F32)
            nc.vector.reciprocal(out=recips[h, a0][:], in_=dens[h, a0][:])

        def finish(h, a0, count, bank, queue):
            res = sbuf("res%d_%d" % (h, a0), [P, count, E], F32)
            n0 = h * (NQ // QT) + a0
            for n in range(count):
                nc.vector.scalar_tensor_tensor(
                    out=res[:, n, :], in0=bank[:, (a0 + n) * E : (a0 + n + 1) * E], scalar=recips[h, a0][:, n : n + 1],
                    in1=gate[:, n0 + n, :], op0=ALU.mult, op1=ALU.mult,
                )
            queue.dma_start(out=out_rows[:, n0 : n0 + count, :], in_=res[:])

        nc.scalar.activation(out=t_rsqrt[:], in_=t_col, func=ACT.Abs_reciprocal_sqrt)
        nc.scalar.activation(out=t_abs[:], in_=t_col, func=ACT.Abs)
        nc.scalar.activation(out=t_sign[:], in_=t_col, func=ACT.Sign)

        nc.scalar.mul(out=bias[:], in_=kb_col, mul=1.0 / CAP)
        nc.scalar.activation(out=gate[:, 0:1, :], in_=og_first[:], func=ACT.Sigmoid)

        ya, yb, yc, yd = y_banks
        S, V = True, False

        interleave_queries(qa16, qa_raw)
        nc.vector.tensor_tensor(out=root[:], in0=t_abs[:], in1=t_rsqrt[:], op=ALU.mult)
        quantise(q_mx, 0, qa16[:])
        nc.vector.tensor_tensor(out=near_one[:], in0=root[:], in1=t_rsqrt[:], op=ALU.mult)
        nc.vector.tensor_scalar(out=polish[:], in0=near_one[:], scalar1=-CAP / 2, scalar2=3 * CAP / 2, op0=ALU.mult, op1=ALU.add)
        nc.vector.tensor_tensor(out=factor[:], in0=root[:], in1=polish[:], op=ALU.mult)
        deal_keys(0, k0_raw, 0, 2)
        quantise_keys(0, 0, 1)
        deal_keys(0, k0_raw, 2, 2)
        quantise_keys(0, 1, 1)
        quantise_keys(0, 2, 2)
        interleave_queries(qb16, qb_raw)
        quantise(q_mx, Q_HALF, qb16[:])
        for a0, groups in ((0, ((0,), (1,), (2, 3))), (2, ((0, 1), (2, 3)))):
            for rs in groups:
                for h in range(H):
                    cap_scores(0, h, rs, a0, 2)
        relu_scale((0, 0), (0, 1))
        deal_keys(1, k1_raw, 0, 4)
        relu_scale((0, 0), (2,))
        quantise_keys(1, 0, 4)
        for r in range(PACK):
            for h in range(H):
                cap_scores(1, h, (r,), 0, 4)
        relu_scale((0, 0), (3,))
        relu_scale((0, 1), (0,))
        square(V, 0, 0, 0, 2)
        relu_scale((0, 1), (1, 2, 3))
        sign_values(0, 0)
        sign_values(0, 1)
        relu_scale((1, 0), (0,))
        sign_values(1, 0)
        relu_scale((1, 0), (1,))
        sign_values(1, 1)
        relu_scale((1, 0), (2, 3))
        square(S, 0, 0, 2, 2)
        square(S, 0, 1, 0, 2)
        square(S, 1, 0, 2, 2)
        square(S, 1, 1, 0, 2)
        quantise(v_mx, 0, v16[:])
        square(V, 1, 0, 0, 2)
        quantise_weights(0, 0, 0, 4)
        quantise_weights(1, 0, 0, 2)
        weigh_values(0, 0, 2, ya)
        quantise_weights(0, 0, 2, 2)
        quantise_weights(1, 0, 2, 2)
        weigh_values(0, 2, 2, yb)
        gates(1, 2)
        square(S, 0, 1, 2, 2)
        quantise_weights(1, 1, 0, 2)
        weigh_values(1, 0, 2, yc)
        denominators(0, 0, 2, ya)
        square(V, 1, 1, 3, 1)
        square(S, 1, 1, 2, 1)
        gates(2, 4)
        gates(4, 8)
        reciprocals(0, 0)
        denominators(0, 2, 2, yb)
        finish(0, 0, 2, ya, nc.sync)
        quantise_weights(0, 1, 2, 2)
        weigh_values(1, 2, 1, yd, (0,))
        weigh_values(1, 3, 1, ya, (0,))
        reciprocals(0, 2)
        denominators(1, 0, 2, yc)
        quantise_weights(1, 1, 2, 2)
        weigh_values(1, 2, 1, yd, (1,))
        weigh_values(1, 3, 1, ya, (1,))
        reciprocals(1, 0)
        finish(0, 2, 2, yb, nc.sync)
        finish(1, 0, 2, yc, nc.sync)
        denominators(1, 2, 1, yd)
        denominators(1, 3, 1, ya)
        reciprocals(1, 2)
        reciprocals(1, 3)
        finish(1, 2, 1, yd, nc.sync)
        finish(1, 3, 1, ya, nc.scalar)
